import numpy as np
import ml_dtypes


def mxq(x, axis, fmt="e4m3"):
    dtype, down = {"e4m3": (ml_dtypes.float8_e4m3fn, 7), "e5m2": (ml_dtypes.float8_e5m2, 14)}[fmt]
    v = np.moveaxis(np.asarray(x, np.float32).astype(ml_dtypes.bfloat16).astype(np.float64), axis, -1)
    blocks = v.reshape(v.shape[:-1] + (-1, 32))
    amax = np.abs(blocks).max(-1, keepdims=True)
    byte = np.maximum(np.where(amax > 0, np.frexp(amax)[1] - 1 + 127, 0) - down, 1)
    scale = np.exp2(byte - 127.0)
    codes = (blocks / scale).astype(np.float32).astype(dtype).astype(np.float64)
    return np.moveaxis((codes * scale).reshape(v.shape), -1, axis)


WIDE = False


def mx_kscale(k):
    if not WIDE:
        return np.ones(k)
    levels = np.array([10, -10, 5, -5, 0])
    if k % 512:
        return np.exp2(np.random.permutation(np.resize(levels, k // 32))).repeat(32)
    a = np.empty((k // 512, 16))
    for p in range(k // 512):
        a[p, :8] = np.random.permutation(np.resize(levels, 8))
        for g in range(8):
            far = levels[np.abs(levels - a[p, g]) >= 10]
            a[p, g + 8] = far[np.random.randint(len(far))]
    return np.exp2(a.ravel()).repeat(32)


def f64(x):
    return np.asarray(x).astype(np.float64)


def striped(idx):
    return np.tile(np.asarray(idx).reshape(-1, 16).T, (8, 1)).astype(np.uint16)


def unstriped(offs):
    return offs[:16].T.reshape(-1).astype(np.int64)


E2M1 = np.array([0.0, 0.5, 1.0, 1.5, 2.0, 3.0, 4.0, 6.0, -0.0, -0.5, -1.0, -1.5, -2.0, -3.0, -4.0, -6.0])


def pack_weight(w, fmt):
    k, n = w.shape
    w = f64(np.asarray(w, np.float32).astype(ml_dtypes.bfloat16)).reshape(k // 32, 32, n)
    amax = np.abs(w).max(1)
    if fmt == "e4m3":
        byte = np.frexp(amax)[1] - 1 + 127 - 7
    else:
        mant, ex = np.frexp(amax / 6.0)
        byte = np.where(mant > 0.5, ex, ex - 1) + 127
    byte = np.clip(np.where(amax > 0, byte, 1), 1, 254)
    scaled = (w * np.exp2(127.0 - byte)[:, None, :]).reshape(k, n).astype(np.float32)
    by_word = np.ascontiguousarray(scaled.reshape(k // 512, 128, 4, n).transpose(0, 1, 3, 2))
    if fmt == "e4m3":
        words = by_word.astype(ml_dtypes.float8_e4m3fn).view(np.uint8)
    else:
        c = by_word.astype(ml_dtypes.float4_e2m1fn).view(np.uint8) & 0xF
        words = (c[..., 0::2] | (c[..., 1::2] << 4)).reshape(k // 512, 128, 2 * n)
    return np.ascontiguousarray(words), np.ascontiguousarray(byte.astype(np.uint8).reshape(k // 512, 16, n))


def unpack_weight(words, scales, fmt):
    g, _, n = scales.shape
    words = np.ascontiguousarray(words).reshape(g, 128, n, -1)
    if fmt == "e4m3":
        vals = words.view(ml_dtypes.float8_e4m3fn).astype(np.float64)
    else:
        nib = np.empty((g, 128, n, 4), np.uint8)
        nib[..., 0::2] = words & 0xF
        nib[..., 1::2] = words >> 4
        vals = E2M1[nib]
    vals = vals * np.repeat(np.exp2(scales.astype(np.float64) - 127.0), 8, axis=1)[..., None]
    return vals.transpose(0, 1, 3, 2).reshape(g * 512, n)


D, T, I, Q, J, G, M = 512, 2048, 512, 128, 512, 64, 2048


def setup_inputs():
    n = np.random.standard_normal
    idx = np.random.permutation(T)[:I]
    idx2 = np.random.permutation(T)[:J]
    idx3 = np.random.permutation(M)[:I]
    fd = mx_kscale(D)
    fj = mx_kscale(J)
    keysp = pack_weight(n((D, T)) / fd[:, None], "e4m3")
    return {
        "query": (n((D, Q)) * 0.6 / np.sqrt(D) * fd[:, None]).astype(np.float32),
        "keys_words": keysp[0],
        "keys_scales": keysp[1],
        "hf": (np.random.uniform(0.5, 2.0, (J, 1)) * fj[:, None]).astype(np.float32),
        "mixer": (n((J, I)) * 0.05 / fj[:, None]).astype(np.float32),
        "cap": (np.random.uniform(0.01, 0.018, (Q, 1))).astype(np.float32),
        "old": (np.random.uniform(0.0, 2.0, (Q, M))).astype(np.float32),
        "fade": (np.random.uniform(0.3, 0.9, (Q, 1))).astype(np.float32),
        "offs": striped(idx),
        "offs2": striped(idx2),
        "offs3": striped(idx3),
    }


def reference(query, keys_words, keys_scales, hf, mixer, cap, old, fade, offs, offs2, offs3):
    idx = unstriped(offs)
    idx2 = unstriped(offs2)
    idx3 = unstriped(offs3)
    keysu = unpack_weight(keys_words, keys_scales, "e4m3")
    keysidx2g = keysu[:, idx2]
    queryq = mxq(f64(query), 0, "e4m3")
    a0 = keysidx2g.T @ queryq
    af = a0 * f64(hf)
    afq = mxq(af, 0, "e4m3")
    mixerq = mxq(f64(mixer), 0, "e4m3")
    mx0 = afq.T @ mixerq
    keysidxg = keysu[:, idx]
    a = queryq.T @ keysidxg
    s = a + mx0
    p = np.exp(s - np.max(s, axis=1, keepdims=True))
    r = p / np.sum(p, axis=1, keepdims=True)
    pg = r.reshape(Q, G, I // G).sum(axis=2)
    k0 = np.minimum(pg, f64(cap)) / pg
    kr = np.repeat(k0, I // G, axis=1)
    w = r * kr
    ws = w * 512.0
    wf = np.zeros((Q, M))
    wf[:, idx3] = ws
    y = f64(old) * f64(fade) + wf
    return y

@@ -1,0 +1,222 @@
+from contextlib import ExitStack
+
+import concourse.mybir as mybir
+
+F32 = mybir.dt.float32
+BF16 = mybir.dt.bfloat16
+I32 = mybir.dt.int32
+U32 = mybir.dt.uint32
+U16 = mybir.dt.uint16
+U8 = mybir.dt.uint8
+FP8X4 = mybir.dt.float8_e4m3fn_x4
+ALU = mybir.AluOpType
+ACT = mybir.ActivationFunctionType
+AXIS = mybir.AxisListType
+
+P = 128
+PACK = 4
+D, T, I, Q, J, G, M = 512, 2048, 512, 128, 512, 64, 2048
+RUN = I // G
+FLOPS = 2 * D * J * Q + 2 * J * Q * I + 2 * D * Q * I
+
+MIXER_CHUNKS = (slice(0, 256), slice(256, 384), slice(384, 512))
+OUT_CHUNKS = (256, 512, 512, 512, 256)
+
+
+def interleave(engine_copy, dst, src):
+    engine_copy(
+        out=dst.rearrange("p (c i) t -> p c t i", i=4),
+        in_=src.rearrange("p t (c i) -> p c t i", i=4),
+    )
+
+
+def tile_attend_mixedslots_runcap_counts_kernel(
+    tc, query, keys_words, keys_scales, hf, mixer, cap, old, fade, offs, offs2, offs3, out
+):
+    nc = tc.nc
+    with ExitStack() as ctx:
+        lists = ctx.enter_context(tc.tile_pool(name="lists", bufs=1))
+        sb = ctx.enter_context(tc.tile_pool(name="sb", bufs=1))
+        psum = ctx.enter_context(tc.psum_pool(name="psum", bufs=1))
+
+        slot_list = lists.tile([P, I // 16], U16, name="slot_list")
+        mixed_list = lists.tile([P, J // 16], U16, name="mixed_list")
+        place_list = lists.tile([P, I // 16], U16, name="place_list")
+
+        pool_scales = sb.tile([P, T], U8, name="pool_scales", align_bytes=64)
+        pool_words = sb.tile([P, T], U32, name="pool_words", align_bytes=64)
+        placed = sb.tile([P, M], F32, name="placed")
+        nc.vector.memset(pool_scales[:].bitcast(I32), 0)
+        nc.vector.memset(placed[:], 0.0)
+
+        query_raw = sb.tile([P, PACK, Q], F32, name="query_raw")
+        nc.sync.dma_start(mixed_list[:], offs2)
+        nc.sync.dma_start(query_raw[:], query.rearrange("(p t) q -> p t q", t=PACK))
+        nc.sync.dma_start(slot_list[:], offs)
+        for r in range(4):
+            nc.sync.dma_start(pool_scales[r:P:32, :].bitcast(I32), keys_scales[0, r:16:4, :].bitcast(I32))
+        nc.sync.dma_start(
+            pool_words[:].bitcast(I32), keys_words[0].rearrange("p n t -> p (n t)").bitcast(I32)
+        )
+        mixer_rows = mixer.rearrange("(p t) i -> p t i", t=PACK)
+        mixer_raw = []
+        hf_sb = sb.tile([P, PACK], F32, name="hf_sb")
+        for c, cols in enumerate(MIXER_CHUNKS):
+            chunk = sb.tile([P, PACK, cols.stop - cols.start], F32, name=f"mixer_raw{c}")
+            nc.sync.dma_start(chunk[:], mixer_rows[:, :, cols])
+            mixer_raw.append(chunk)
+            if c == 0:
+                nc.sync.dma_start(hf_sb[:], hf.rearrange("(p t) o -> p (t o)", t=PACK))
+        cap_sb = sb.tile([P, 1], F32, name="cap_sb")
+        fade_sb = sb.tile([P, 1], F32, name="fade_sb")
+        old_sb = sb.tile([P, M], F32, name="old_sb")
+        nc.sync.dma_start(cap_sb[:], cap)
+        nc.sync.dma_start(place_list[:], offs3)
+        nc.sync.dma_start(fade_sb[:], fade)
+        nc.sync.dma_start(old_sb[:], old)
+
+        query_bf = sb.tile([P, Q, PACK], BF16, name="query_bf", align_bytes=64)
+        query_words = sb.tile([P, Q], U32, name="query_words", align_bytes=64)
+        query_scales = sb.tile([P, Q], U8, name="query_scales", align_bytes=64)
+        interleave(nc.scalar.copy, query_bf[:], query_raw[:])
+
+        mixed_words = sb.tile([P, J], U32, name="mixed_words", align_bytes=64)
+        mixed_scales = sb.tile([P, J], U8, name="mixed_scales", align_bytes=64)
+        slot_words = sb.tile([P, I], U32, name="slot_words", align_bytes=64)
+        slot_scales = sb.tile([P, I], U8, name="slot_scales", align_bytes=64)
+        nc.vector.tensor_copy(
+            mixed_scales[:].rearrange("p (t m) -> p m t", t=PACK), pool_scales[:].indirect(mixed_list[:])
+        )
+        nc.vector.quantize_mx(
+            out=query_words[:].bitcast(FP8X4),
+            scales=query_scales[:],
+            in_=query_bf[:].rearrange("p q t -> p (q t)"),
+        )
+        nc.vector.tensor_copy(slot_scales[:], pool_scales[:].indirect(slot_list[:]))
+        nc.vector.tensor_copy(
+            mixed_words[:].rearrange("p (t m) -> p m t", t=PACK), pool_words[:].indirect(mixed_list[:])
+        )
+
+        a0 = psum.tile([P, PACK, Q], F32, name="a0")
+        for t in range(PACK):
+            cols = slice(t * P, (t + 1) * P)
+            nc.tensor.matmul_mx(
+                out=a0[:, t, :],
+                lhsT=mixed_words[:, cols].bitcast(FP8X4),
+                lhsT_scale=mixed_scales[:, cols],
+                rhs=query_words[:].bitcast(FP8X4),
+                rhs_scale=query_scales[:],
+                start=True,
+                stop=True,
+            )
+        nc.vector.tensor_copy(slot_words[:], pool_words[:].indirect(slot_list[:]))
+
+        scores = psum.tile([P, I], F32, name="scores")
+        nc.tensor.matmul_mx(
+            out=scores[:],
+            lhsT=query_words[:].bitcast(FP8X4),
+            lhsT_scale=query_scales[:],
+            rhs=slot_words[:].bitcast(FP8X4),
+            rhs_scale=slot_scales[:],
+            start=True,
+            stop=False,
+        )
+
+        af_bf = sb.tile([P, Q, PACK], BF16, name="af_bf", align_bytes=64)
+        af_words = sb.tile([P, Q], U32, name="af_words", align_bytes=64)
+        af_scales = sb.tile([P, Q], U8, name="af_scales", align_bytes=64)
+        nc.vector.tensor_tensor(
+            af_bf[:],
+            a0[:].rearrange("p t q -> p q t"),
+            hf_sb[:].unsqueeze(1).to_broadcast([P, Q, PACK]),
+            ALU.mult,
+        )
+
+        mixer_bf = sb.tile([P, I, PACK], BF16, name="mixer_bf", align_bytes=64)
+        mixer_words = sb.tile([P, I], U32, name="mixer_words", align_bytes=64)
+        mixer_scales = sb.tile([P, I], U8, name="mixer_scales", align_bytes=64)
+        for c, cols in enumerate(MIXER_CHUNKS):
+            interleave(nc.scalar.copy, mixer_bf[:, cols, :], mixer_raw[c][:])
+
+        def quantise_mixer(cols):
+            nc.vector.quantize_mx(
+                out=mixer_words[:, cols].bitcast(FP8X4),
+                scales=mixer_scales[:, cols],
+                in_=mixer_bf[:, cols, :].rearrange("p i t -> p (i t)"),
+            )
+
+        quantise_mixer(slice(0, I // 2))
+        nc.vector.quantize_mx(
+            out=af_words[:].bitcast(FP8X4),
+            scales=af_scales[:],
+            in_=af_bf[:].rearrange("p q t -> p (q t)"),
+        )
+        quantise_mixer(slice(I // 2, I))
+        for h in range(2):
+            cols = slice(h * I // 2, (h + 1) * I // 2)
+            nc.tensor.matmul_mx(
+                out=scores[:, cols],
+                lhsT=af_words[:].bitcast(FP8X4),
+                lhsT_scale=af_scales[:],
+                rhs=mixer_words[:, cols].bitcast(FP8X4),
+                rhs_scale=mixer_scales[:, cols],
+                start=False,
+                stop=(h == 1),
+            )
+
+        cap512 = sb.tile([P, 1], F32, name="cap512")
+        nc.scalar.activation(cap512[:], cap_sb[:], ACT.Copy, scale=512.0)
+        neg_max = sb.tile([P, 1], F32, name="neg_max")
+        nc.vector.tensor_reduce(neg_max[:], scores[:], AXIS.X, ALU.max, negate=True)
+        p = sb.tile([P, I], F32, name="p")
+        run_sums = sb.tile([P, G], F32, name="run_sums")
+        half_sums = [sb.tile([P, 1], F32, name=f"half_sum{h}") for h in range(2)]
+        for h in range(2):
+            cols = slice(h * I // 2, (h + 1) * I // 2)
+            nc.scalar.activation(p[:, cols], scores[:, cols], ACT.Exp, bias=neg_max[:], accum_out=half_sums[h][:])
+            nc.vector.tensor_reduce(
+                run_sums[:, h * G // 2 : (h + 1) * G // 2],
+                p[:, cols].rearrange("p (g r) -> p g r", r=RUN),
+                AXIS.X,
+                ALU.add,
+            )
+        first_share = sb.tile([P, 1], F32, name="first_share")
+        row_share = sb.tile([P, 1], F32, name="row_share")
+        nc.scalar.activation(first_share[:], half_sums[0][:], ACT.Copy, scale=1.0 / 512.0)
+        nc.scalar.activation(row_share[:], half_sums[1][:], ACT.Identity, scale=1.0 / 512.0, bias=first_share[:])
+
+        inverse_run = sb.tile([P, G], F32, name="inverse_run")
+        inverse_row = sb.tile([P, 1], F32, name="inverse_row")
+        factor = sb.tile([P, I], F32, name="factor")
+        nc.vector.reciprocal(inverse_run[:, : G // 2], run_sums[:, : G // 2])
+        nc.vector.reciprocal(inverse_row[:], row_share[:])
+        nc.vector.reciprocal(inverse_run[:, G // 2 :], run_sums[:, G // 2 :])
+        for h in range(2):
+            runs = slice(h * G // 2, (h + 1) * G // 2)
+            cols = slice(h * I // 2, (h + 1) * I // 2)
+            nc.vector.tensor_scalar(
+                factor[:, cols].rearrange("p (g r) -> p g r", r=RUN),
+                inverse_run[:, runs].unsqueeze(2).to_broadcast([P, G // 2, RUN]),
+                cap512[:],
+                inverse_row[:],
+                ALU.mult,
+                ALU.min,
+            )
+        for h in range(2):
+            cols = slice(h * I // 2, (h + 1) * I // 2)
+            nc.vector.tensor_tensor(
+                placed[:].indirect(place_list[:, h * I // 32 : (h + 1) * I // 32]),
+                p[:, cols],
+                factor[:, cols],
+                ALU.mult,
+            )
+
+        start = 0
+        for c, width in enumerate(OUT_CHUNKS):
+            cols = slice(start, start + width)
+            start = start + width
+            result = sb.tile([P, width], F32, name=f"result{c}")
+            nc.vector.scalar_tensor_tensor(
+                result[:], old_sb[:, cols], fade_sb[:], placed[:, cols], ALU.mult, ALU.add
+            )
+            nc.sync.dma_start(out[:, cols], result[:])

@@ -50,17 +50,17 @@ def tile_attend_mixedslots_runcap_counts_kernel(
         nc.vector.memset(placed[:], 0.0)
 
         query_raw = sb.tile([P, PACK, Q], F32, name="query_raw")
-        nc.sync.dma_start(mixed_list[:], offs2)
         nc.sync.dma_start(query_raw[:], query.rearrange("(p t) q -> p t q", t=PACK))
+        nc.sync.dma_start(mixed_list[:], offs2)
         nc.sync.dma_start(slot_list[:], offs)
         for r in range(4):
             nc.sync.dma_start(pool_scales[r:P:32, :].bitcast(I32), keys_scales[0, r:16:4, :].bitcast(I32))
         nc.sync.dma_start(
             pool_words[:].bitcast(I32), keys_words[0].rearrange("p n t -> p (n t)").bitcast(I32)
         )
+        hf_sb = sb.tile([P, PACK], F32, name="hf_sb")
         mixer_rows = mixer.rearrange("(p t) i -> p t i", t=PACK)
         mixer_raw = []
-        hf_sb = sb.tile([P, PACK], F32, name="hf_sb")
         for c, cols in enumerate(MIXER_CHUNKS):
             chunk = sb.tile([P, PACK, cols.stop - cols.start], F32, name=f"mixer_raw{c}")
             nc.sync.dma_start(chunk[:], mixer_rows[:, :, cols])
@@ -78,19 +78,18 @@ def tile_attend_mixedslots_runcap_counts_kernel(
         query_bf = sb.tile([P, Q, PACK], BF16, name="query_bf", align_bytes=64)
         query_words = sb.tile([P, Q], U32, name="query_words", align_bytes=64)
         query_scales = sb.tile([P, Q], U8, name="query_scales", align_bytes=64)
-        interleave(nc.scalar.copy, query_bf[:], query_raw[:])
-
-        mixed_words = sb.tile([P, J], U32, name="mixed_words", align_bytes=64)
-        mixed_scales = sb.tile([P, J], U8, name="mixed_scales", align_bytes=64)
-        slot_words = sb.tile([P, I], U32, name="slot_words", align_bytes=64)
-        slot_scales = sb.tile([P, I], U8, name="slot_scales", align_bytes=64)
-        nc.vector.tensor_copy(
-            mixed_scales[:].rearrange("p (t m) -> p m t", t=PACK), pool_scales[:].indirect(mixed_list[:])
-        )
+        interleave(nc.vector.tensor_copy, query_bf[:], query_raw[:])
         nc.vector.quantize_mx(
             out=query_words[:].bitcast(FP8X4),
             scales=query_scales[:],
             in_=query_bf[:].rearrange("p q t -> p (q t)"),
+        )
+
+        mixed_words = sb.tile([P, J], U32, name="mixed_words", align_bytes=64)
+        mixed_scales = sb.tile([P, J], U8, name="mixed_scales", align_bytes=64)
+        slot_scales = sb.tile([P, I], U8, name="slot_scales", align_bytes=64)
+        nc.vector.tensor_copy(
+            mixed_scales[:].rearrange("p (t m) -> p m t", t=PACK), pool_scales[:].indirect(mixed_list[:])
         )
         nc.vector.tensor_copy(slot_scales[:], pool_scales[:].indirect(slot_list[:]))
         nc.vector.tensor_copy(
@@ -109,18 +108,21 @@ def tile_attend_mixedslots_runcap_counts_kernel(
                 start=True,
                 stop=True,
             )
+        slot_words = sb.tile([P, I], U32, name="slot_words", align_bytes=64)
         nc.vector.tensor_copy(slot_words[:], pool_words[:].indirect(slot_list[:]))
 
-        scores = psum.tile([P, I], F32, name="scores")
-        nc.tensor.matmul_mx(
-            out=scores[:],
-            lhsT=query_words[:].bitcast(FP8X4),
-            lhsT_scale=query_scales[:],
-            rhs=slot_words[:].bitcast(FP8X4),
-            rhs_scale=slot_scales[:],
-            start=True,
-            stop=False,
-        )
+        halves = (slice(0, I // 2), slice(I // 2, I))
+        scores = [psum.tile([P, I // 2], F32, name=f"scores{h}") for h in range(2)]
+        for h, cols in enumerate(halves):
+            nc.tensor.matmul_mx(
+                out=scores[h][:],
+                lhsT=query_words[:].bitcast(FP8X4),
+                lhsT_scale=query_scales[:],
+                rhs=slot_words[:, cols].bitcast(FP8X4),
+                rhs_scale=slot_scales[:, cols],
+                start=True,
+                stop=False,
+            )
 
         af_bf = sb.tile([P, Q, PACK], BF16, name="af_bf", align_bytes=64)
         af_words = sb.tile([P, Q], U32, name="af_words", align_bytes=64)
@@ -145,35 +147,43 @@ def tile_attend_mixedslots_runcap_counts_kernel(
                 in_=mixer_bf[:, cols, :].rearrange("p i t -> p (i t)"),
             )
 
-        quantise_mixer(slice(0, I // 2))
+        quantise_mixer(MIXER_CHUNKS[0])
         nc.vector.quantize_mx(
             out=af_words[:].bitcast(FP8X4),
             scales=af_scales[:],
             in_=af_bf[:].rearrange("p q t -> p (q t)"),
         )
-        quantise_mixer(slice(I // 2, I))
-        for h in range(2):
-            cols = slice(h * I // 2, (h + 1) * I // 2)
+        for cols in MIXER_CHUNKS[1:]:
+            quantise_mixer(cols)
+        for cols in MIXER_CHUNKS:
+            h, first = divmod(cols.start, I // 2)
             nc.tensor.matmul_mx(
-                out=scores[:, cols],
+                out=scores[h][:, first : first + cols.stop - cols.start],
                 lhsT=af_words[:].bitcast(FP8X4),
                 lhsT_scale=af_scales[:],
                 rhs=mixer_words[:, cols].bitcast(FP8X4),
                 rhs_scale=mixer_scales[:, cols],
                 start=False,
-                stop=(h == 1),
+                stop=(cols.stop == halves[h].stop),
             )
 
         cap512 = sb.tile([P, 1], F32, name="cap512")
         nc.scalar.activation(cap512[:], cap_sb[:], ACT.Copy, scale=512.0)
+        neg_first_max = sb.tile([P, 1], F32, name="neg_first_max")
         neg_max = sb.tile([P, 1], F32, name="neg_max")
-        nc.vector.tensor_reduce(neg_max[:], scores[:], AXIS.X, ALU.max, negate=True)
+        neg_scores = sb.tile([P, I // 2], F32, name="neg_scores")
+        nc.vector.tensor_reduce(neg_first_max[:], scores[0][:], AXIS.X, ALU.max, negate=True)
+        nc.vector.tensor_scalar(
+            neg_scores[:], scores[1][:], -1.0, neg_first_max[:], ALU.mult, ALU.min, accum_out=neg_max[:]
+        )
         p = sb.tile([P, I], F32, name="p")
         run_sums = sb.tile([P, G], F32, name="run_sums")
         half_sums = [sb.tile([P, 1], F32, name=f"half_sum{h}") for h in range(2)]
-        for h in range(2):
-            cols = slice(h * I // 2, (h + 1) * I // 2)
-            nc.scalar.activation(p[:, cols], scores[:, cols], ACT.Exp, bias=neg_max[:], accum_out=half_sums[h][:])
+        for h, (source, sign) in enumerate(((scores[0], 1.0), (neg_scores, -1.0))):
+            cols = halves[h]
+            nc.scalar.activation(
+                p[:, cols], source[:], ACT.Exp, scale=sign, bias=neg_max[:], accum_out=half_sums[h][:]
+            )
             nc.vector.tensor_reduce(
                 run_sums[:, h * G // 2 : (h + 1) * G // 2],
                 p[:, cols].rearrange("p (g r) -> p g r", r=RUN),

@@ -1,6 +1,7 @@
 from contextlib import ExitStack
 
 import concourse.mybir as mybir
+from concourse.masks import make_identity
 
 F32 = mybir.dt.float32
 BF16 = mybir.dt.bfloat16
@@ -15,12 +16,29 @@ AXIS = mybir.AxisListType
 
 P = 128
 PACK = 4
+ENTRIES = 16
+QUADRANT = 32
 D, T, I, Q, J, G, M = 512, 2048, 512, 128, 512, 64, 2048
 RUN = I // G
+WEIGHT_SCALE = 512.0
 FLOPS = 2 * D * J * Q + 2 * J * Q * I + 2 * D * Q * I
 
-MIXER_CHUNKS = (slice(0, 256), slice(256, 384), slice(384, 512))
-OUT_CHUNKS = (256, 512, 512, 512, 256)
+
+def spans(first, widths):
+    return [slice(first + sum(widths[:c]), first + sum(widths[: c + 1])) for c in range(len(widths))]
+
+
+SLOT_HALVES = spans(0, (I // 2, I // 2))
+RUN_HALVES = spans(0, (G // 2, G // 2))
+MIXER_CHUNKS = spans(0, (256, 128, 128))
+PLAIN_CHUNKS = spans(0, (128, 384, 512))
+PLAIN_COLS = PLAIN_CHUNKS[-1].stop
+TURNED_CHUNKS = spans(PLAIN_COLS, (256, 256, 256, 256))
+FADED_PIECES = spans(PLAIN_COLS, (512, 512))
+
+
+def width(cols):
+    return cols.stop - cols.start
 
 
 def interleave(engine_copy, dst, src):
@@ -37,56 +55,75 @@ def tile_attend_mixedslots_runcap_counts_kernel(
     with ExitStack() as ctx:
         lists = ctx.enter_context(tc.tile_pool(name="lists", bufs=1))
         sb = ctx.enter_context(tc.tile_pool(name="sb", bufs=1))
+        reused = ctx.enter_context(tc.tile_pool(name="reused", bufs=1))
         psum = ctx.enter_context(tc.psum_pool(name="psum", bufs=1))
 
-        slot_list = lists.tile([P, I // 16], U16, name="slot_list")
-        mixed_list = lists.tile([P, J // 16], U16, name="mixed_list")
-        place_list = lists.tile([P, I // 16], U16, name="place_list")
+        def quantise(words, scales, interleaved):
+            nc.vector.quantize_mx(
+                out=words.bitcast(FP8X4), scales=scales, in_=interleaved.rearrange("p c t -> p (c t)")
+            )
+
+        def multiply(bank, lhs_words, lhs_scales, rhs_words, rhs_scales, start, stop):
+            nc.tensor.matmul_mx(
+                out=bank,
+                lhsT=lhs_words.bitcast(FP8X4),
+                lhsT_scale=lhs_scales,
+                rhs=rhs_words.bitcast(FP8X4),
+                rhs_scale=rhs_scales,
+                start=start,
+                stop=stop,
+            )
+
+        slot_list = lists.tile([P, I // ENTRIES], U16, name="slot_list")
+        mixed_list = lists.tile([P, J // ENTRIES], U16, name="mixed_list")
+        place_list = lists.tile([P, I // ENTRIES], U16, name="place_list")
 
         pool_scales = sb.tile([P, T], U8, name="pool_scales", align_bytes=64)
         pool_words = sb.tile([P, T], U32, name="pool_words", align_bytes=64)
-        placed = sb.tile([P, M], F32, name="placed")
+        vector_window = sb.tile([P, M], F32, name="vector_window")
+        identity = sb.tile([P, P], F32, name="identity")
         nc.vector.memset(pool_scales[:].bitcast(I32), 0)
-        nc.vector.memset(placed[:], 0.0)
+        nc.vector.memset(identity[:], 0.0)
+        make_identity(nc, identity[:], nomemset=True)
+        nc.vector.memset(vector_window[:], 0.0)
 
         query_raw = sb.tile([P, PACK, Q], F32, name="query_raw")
         nc.sync.dma_start(query_raw[:], query.rearrange("(p t) q -> p t q", t=PACK))
         nc.sync.dma_start(mixed_list[:], offs2)
         nc.sync.dma_start(slot_list[:], offs)
         for r in range(4):
-            nc.sync.dma_start(pool_scales[r:P:32, :].bitcast(I32), keys_scales[0, r:16:4, :].bitcast(I32))
+            nc.sync.dma_start(pool_scales[r:P:QUADRANT, :].bitcast(I32), keys_scales[0, r:16:4, :].bitcast(I32))
         nc.sync.dma_start(
             pool_words[:].bitcast(I32), keys_words[0].rearrange("p n t -> p (n t)").bitcast(I32)
         )
         hf_sb = sb.tile([P, PACK], F32, name="hf_sb")
+        nc.sync.dma_start(hf_sb[:], hf.rearrange("(p t) o -> p (t o)", t=PACK))
         mixer_rows = mixer.rearrange("(p t) i -> p t i", t=PACK)
         mixer_raw = []
         for c, cols in enumerate(MIXER_CHUNKS):
-            chunk = sb.tile([P, PACK, cols.stop - cols.start], F32, name=f"mixer_raw{c}")
+            chunk = sb.tile([P, PACK, width(cols)], F32, name=f"mixer_raw{c}")
             nc.sync.dma_start(chunk[:], mixer_rows[:, :, cols])
             mixer_raw.append(chunk)
-            if c == 0:
-                nc.sync.dma_start(hf_sb[:], hf.rearrange("(p t) o -> p (t o)", t=PACK))
         cap_sb = sb.tile([P, 1], F32, name="cap_sb")
         fade_sb = sb.tile([P, 1], F32, name="fade_sb")
-        old_sb = sb.tile([P, M], F32, name="old_sb")
-        nc.sync.dma_start(cap_sb[:], cap)
-        nc.sync.dma_start(place_list[:], offs3)
+        old_plain = sb.tile([P, PLAIN_COLS], F32, name="old_plain")
+        old_turned = [sb.tile([P, width(cols)], F32, name=f"old_turned{h}") for h, cols in enumerate(FADED_PIECES)]
         nc.sync.dma_start(fade_sb[:], fade)
-        nc.sync.dma_start(old_sb[:], old)
+        nc.sync.dma_start(old_turned[0][:], old[:, FADED_PIECES[0]])
+        nc.sync.dma_start(cap_sb[:], cap)
+        nc.sync.dma_start(old_turned[1][:], old[:, FADED_PIECES[1]])
+        nc.sync.dma_start(place_list[:], offs3)
+        nc.sync.dma_start(old_plain[:], old[:, :PLAIN_COLS])
 
         query_bf = sb.tile([P, Q, PACK], BF16, name="query_bf", align_bytes=64)
         query_words = sb.tile([P, Q], U32, name="query_words", align_bytes=64)
         query_scales = sb.tile([P, Q], U8, name="query_scales", align_bytes=64)
         interleave(nc.vector.tensor_copy, query_bf[:], query_raw[:])
-        nc.vector.quantize_mx(
-            out=query_words[:].bitcast(FP8X4),
-            scales=query_scales[:],
-            in_=query_bf[:].rearrange("p q t -> p (q t)"),
-        )
+        quantise(query_words[:], query_scales[:], query_bf[:])
 
         mixed_words = sb.tile([P, J], U32, name="mixed_words", align_bytes=64)
         mixed_scales = sb.tile([P, J], U8, name="mixed_scales", align_bytes=64)
+        slot_words = sb.tile([P, I], U32, name="slot_words", align_bytes=64)
         slot_scales = sb.tile([P, I], U8, name="slot_scales", align_bytes=64)
         nc.vector.tensor_copy(
             mixed_scales[:].rearrange("p (t m) -> p m t", t=PACK), pool_scales[:].indirect(mixed_list[:])
@@ -95,37 +132,20 @@ def tile_attend_mixedslots_runcap_counts_kernel(
         nc.vector.tensor_copy(
             mixed_words[:].rearrange("p (t m) -> p m t", t=PACK), pool_words[:].indirect(mixed_list[:])
         )
-
-        a0 = psum.tile([P, PACK, Q], F32, name="a0")
-        for t in range(PACK):
-            cols = slice(t * P, (t + 1) * P)
-            nc.tensor.matmul_mx(
-                out=a0[:, t, :],
-                lhsT=mixed_words[:, cols].bitcast(FP8X4),
-                lhsT_scale=mixed_scales[:, cols],
-                rhs=query_words[:].bitcast(FP8X4),
-                rhs_scale=query_scales[:],
-                start=True,
-                stop=True,
+        a0 = psum.tile([P, PACK, Q], F32, name="a0", tag="a0")
+        for t, cols in enumerate(spans(0, (P,) * PACK)):
+            multiply(
+                a0[:, t, :], mixed_words[:, cols], mixed_scales[:, cols], query_words[:], query_scales[:], True, True
             )
-        slot_words = sb.tile([P, I], U32, name="slot_words", align_bytes=64)
         nc.vector.tensor_copy(slot_words[:], pool_words[:].indirect(slot_list[:]))
 
-        halves = (slice(0, I // 2), slice(I // 2, I))
-        scores = [psum.tile([P, I // 2], F32, name=f"scores{h}") for h in range(2)]
-        for h, cols in enumerate(halves):
-            nc.tensor.matmul_mx(
-                out=scores[h][:],
-                lhsT=query_words[:].bitcast(FP8X4),
-                lhsT_scale=query_scales[:],
-                rhs=slot_words[:, cols].bitcast(FP8X4),
-                rhs_scale=slot_scales[:, cols],
-                start=True,
-                stop=False,
+        scores = [psum.tile([P, I // 2], F32, name=f"scores{h}", tag=f"scores{h}") for h in range(2)]
+        for h, cols in enumerate(SLOT_HALVES):
+            multiply(
+                scores[h][:], query_words[:], query_scales[:], slot_words[:, cols], slot_scales[:, cols], True, False
             )
 
         af_bf = sb.tile([P, Q, PACK], BF16, name="af_bf", align_bytes=64)
-        af_words = sb.tile([P, Q], U32, name="af_words", align_bytes=64)
         af_scales = sb.tile([P, Q], U8, name="af_scales", align_bytes=64)
         nc.vector.tensor_tensor(
             af_bf[:],
@@ -134,42 +154,39 @@ def tile_attend_mixedslots_runcap_counts_kernel(
             ALU.mult,
         )
 
-        mixer_bf = sb.tile([P, I, PACK], BF16, name="mixer_bf", align_bytes=64)
+        mixer_bf = [
+            sb.tile([P, width(MIXER_CHUNKS[0]), PACK], BF16, name="mixer_bf0", tag="mixer_bf0", align_bytes=64),
+            sb.tile([P, width(MIXER_CHUNKS[1]), PACK], BF16, name="mixer_bf1", align_bytes=64),
+            reused.tile([P, width(MIXER_CHUNKS[2]), PACK], BF16, name="mixer_bf2", align_bytes=64, offset=0),
+        ]
         mixer_words = sb.tile([P, I], U32, name="mixer_words", align_bytes=64)
         mixer_scales = sb.tile([P, I], U8, name="mixer_scales", align_bytes=64)
-        for c, cols in enumerate(MIXER_CHUNKS):
-            interleave(nc.scalar.copy, mixer_bf[:, cols, :], mixer_raw[c][:])
+        for c in range(len(MIXER_CHUNKS)):
+            interleave(nc.scalar.copy, mixer_bf[c][:], mixer_raw[c][:])
 
-        def quantise_mixer(cols):
-            nc.vector.quantize_mx(
-                out=mixer_words[:, cols].bitcast(FP8X4),
-                scales=mixer_scales[:, cols],
-                in_=mixer_bf[:, cols, :].rearrange("p i t -> p (i t)"),
-            )
-
-        quantise_mixer(MIXER_CHUNKS[0])
-        nc.vector.quantize_mx(
-            out=af_words[:].bitcast(FP8X4),
-            scales=af_scales[:],
-            in_=af_bf[:].rearrange("p q t -> p (q t)"),
-        )
-        for cols in MIXER_CHUNKS[1:]:
-            quantise_mixer(cols)
+        quantise(mixer_words[:, MIXER_CHUNKS[0]], mixer_scales[:, MIXER_CHUNKS[0]], mixer_bf[0][:])
+        af_words = sb.tile([P, Q], U32, name="af_words", tag="mixer_bf0", align_bytes=64)
+        quantise(af_words[:], af_scales[:], af_bf[:])
+        for c in range(1, len(MIXER_CHUNKS)):
+            quantise(mixer_words[:, MIXER_CHUNKS[c]], mixer_scales[:, MIXER_CHUNKS[c]], mixer_bf[c][:])
         for cols in MIXER_CHUNKS:
             h, first = divmod(cols.start, I // 2)
-            nc.tensor.matmul_mx(
-                out=scores[h][:, first : first + cols.stop - cols.start],
-                lhsT=af_words[:].bitcast(FP8X4),
-                lhsT_scale=af_scales[:],
-                rhs=mixer_words[:, cols].bitcast(FP8X4),
-                rhs_scale=mixer_scales[:, cols],
-                start=False,
-                stop=(cols.stop == halves[h].stop),
+            multiply(
+                scores[h][:, first : first + width(cols)],
+                af_words[:],
+                af_scales[:],
+                mixer_words[:, cols],
+                mixer_scales[:, cols],
+                False,
+                cols.stop == SLOT_HALVES[h].stop,
             )
 
-        cap512 = sb.tile([P, 1], F32, name="cap512")
-        nc.scalar.activation(cap512[:], cap_sb[:], ACT.Copy, scale=512.0)
-        neg_first_max = sb.tile([P, 1], F32, name="neg_first_max")
+        scalar_window = reused.tile([P, M], F32, name="scalar_window", align_bytes=64, offset=64)
+        nc.gpsimd.memset(scalar_window[:], 0.0)
+
+        cap_scaled = sb.tile([P, 1], F32, name="cap_scaled")
+        nc.scalar.activation(cap_scaled[:], cap_sb[:], ACT.Copy, scale=WEIGHT_SCALE)
+        neg_first_max = reused.tile([P, 1], F32, name="neg_first_max", align_bytes=64, offset=0)
         neg_max = sb.tile([P, 1], F32, name="neg_max")
         neg_scores = sb.tile([P, I // 2], F32, name="neg_scores")
         nc.vector.tensor_reduce(neg_first_max[:], scores[0][:], AXIS.X, ALU.max, negate=True)
@@ -180,53 +197,111 @@ def tile_attend_mixedslots_runcap_counts_kernel(
         run_sums = sb.tile([P, G], F32, name="run_sums")
         half_sums = [sb.tile([P, 1], F32, name=f"half_sum{h}") for h in range(2)]
         for h, (source, sign) in enumerate(((scores[0], 1.0), (neg_scores, -1.0))):
-            cols = halves[h]
             nc.scalar.activation(
-                p[:, cols], source[:], ACT.Exp, scale=sign, bias=neg_max[:], accum_out=half_sums[h][:]
+                p[:, SLOT_HALVES[h]], source[:], ACT.Exp, scale=sign, bias=neg_max[:], accum_out=half_sums[h][:]
             )
             nc.vector.tensor_reduce(
-                run_sums[:, h * G // 2 : (h + 1) * G // 2],
-                p[:, cols].rearrange("p (g r) -> p g r", r=RUN),
+                run_sums[:, RUN_HALVES[h]],
+                p[:, SLOT_HALVES[h]].rearrange("p (g r) -> p g r", r=RUN),
                 AXIS.X,
                 ALU.add,
             )
-        first_share = sb.tile([P, 1], F32, name="first_share")
+        first_share = sb.tile([P, 1], F32, name="first_share", tag="first_share")
         row_share = sb.tile([P, 1], F32, name="row_share")
-        nc.scalar.activation(first_share[:], half_sums[0][:], ACT.Copy, scale=1.0 / 512.0)
-        nc.scalar.activation(row_share[:], half_sums[1][:], ACT.Identity, scale=1.0 / 512.0, bias=first_share[:])
+        nc.scalar.activation(first_share[:], half_sums[0][:], ACT.Copy, scale=1.0 / WEIGHT_SCALE)
+        nc.scalar.activation(
+            row_share[:], half_sums[1][:], ACT.Identity, scale=1.0 / WEIGHT_SCALE, bias=first_share[:]
+        )
+
+        faded = [
+            sb.tile([P, width(FADED_PIECES[0])], F32, name="faded0"),
+            sb.tile([P, width(FADED_PIECES[1])], F32, name="faded1", tag="first_share"),
+        ]
+        for h in range(2):
+            nc.scalar.activation(faded[h][:], old_turned[h][:], ACT.Copy, scale=fade_sb[:])
+
+        turned_tags = ("turned0", "turned1", "a0", "scores1")
+        back_tags = ("back0", "back1", "back2", "scores0")
+        turned = [
+            psum.tile([P, width(cols)], F32, name=f"turned{c}", tag=turned_tags[c])
+            for c, cols in enumerate(TURNED_CHUNKS)
+        ]
+
+        def add_turned(c, source, first_col, opens):
+            blocks = width(TURNED_CHUNKS[c]) // P
+            for b in range(blocks):
+                col = first_col + b * P
+                nc.tensor.matmul(
+                    turned[c][:, b * P : (b + 1) * P],
+                    source[:, col : col + P],
+                    identity[:],
+                    start=opens and b == 0,
+                    stop=not opens and b == blocks - 1,
+                    is_transpose=True,
+                )
+
+        for c, cols in enumerate(TURNED_CHUNKS):
+            h, first_col = divmod(cols.start - PLAIN_COLS, width(FADED_PIECES[0]))
+            add_turned(c, faded[h], first_col, True)
 
         inverse_run = sb.tile([P, G], F32, name="inverse_run")
         inverse_row = sb.tile([P, 1], F32, name="inverse_row")
-        factor = sb.tile([P, I], F32, name="factor")
-        nc.vector.reciprocal(inverse_run[:, : G // 2], run_sums[:, : G // 2])
+        nc.vector.reciprocal(inverse_run[:, RUN_HALVES[0]], run_sums[:, RUN_HALVES[0]])
         nc.vector.reciprocal(inverse_row[:], row_share[:])
-        nc.vector.reciprocal(inverse_run[:, G // 2 :], run_sums[:, G // 2 :])
-        for h in range(2):
-            runs = slice(h * G // 2, (h + 1) * G // 2)
-            cols = slice(h * I // 2, (h + 1) * I // 2)
-            nc.vector.tensor_scalar(
-                factor[:, cols].rearrange("p (g r) -> p g r", r=RUN),
-                inverse_run[:, runs].unsqueeze(2).to_broadcast([P, G // 2, RUN]),
-                cap512[:],
-                inverse_row[:],
-                ALU.mult,
-                ALU.min,
-            )
-        for h in range(2):
-            cols = slice(h * I // 2, (h + 1) * I // 2)
-            nc.vector.tensor_tensor(
-                placed[:].indirect(place_list[:, h * I // 32 : (h + 1) * I // 32]),
-                p[:, cols],
-                factor[:, cols],
-                ALU.mult,
-            )
+        nc.vector.reciprocal(inverse_run[:, RUN_HALVES[1]], run_sums[:, RUN_HALVES[1]])
+        first_factor = sb.tile([P, G // 2], F32, name="first_factor")
+        first_ws = sb.tile([P, I // 2], F32, name="first_ws")
+        second_factor = sb.tile([P, I // 2], F32, name="second_factor")
+        nc.vector.tensor_scalar(
+            first_factor[:], inverse_run[:, RUN_HALVES[0]], cap_scaled[:], inverse_row[:], ALU.mult, ALU.min
+        )
+        nc.vector.tensor_scalar(
+            second_factor[:].rearrange("p (g r) -> p g r", r=RUN),
+            inverse_run[:, RUN_HALVES[1]].unsqueeze(2).to_broadcast([P, G // 2, RUN]),
+            cap_scaled[:],
+            inverse_row[:],
+            ALU.mult,
+            ALU.min,
+        )
+        nc.vector.tensor_tensor(
+            first_ws[:].rearrange("p (g r) -> p g r", r=RUN),
+            p[:, SLOT_HALVES[0]].rearrange("p (g r) -> p g r", r=RUN),
+            first_factor[:].unsqueeze(2).to_broadcast([P, G // 2, RUN]),
+            ALU.mult,
+        )
+        half_list = I // 2 // ENTRIES
+        nc.scalar.activation(scalar_window[:].indirect(place_list[:, :half_list]), first_ws[:], ACT.Copy)
+        nc.vector.tensor_tensor(
+            vector_window[:].indirect(place_list[:, half_list:]), p[:, SLOT_HALVES[1]], second_factor[:], ALU.mult
+        )
 
-        start = 0
-        for c, width in enumerate(OUT_CHUNKS):
-            cols = slice(start, start + width)
-            start = start + width
-            result = sb.tile([P, width], F32, name=f"result{c}")
-            nc.vector.scalar_tensor_tensor(
-                result[:], old_sb[:, cols], fade_sb[:], placed[:, cols], ALU.mult, ALU.add
-            )
+        for c, cols in enumerate(TURNED_CHUNKS):
+            add_turned(c, scalar_window, cols.start, False)
+        back = []
+        for c, cols in enumerate(TURNED_CHUNKS):
+            staged = sb.tile([P, width(cols)], F32, name=f"staged{c}")
+            nc.scalar.copy(staged[:], turned[c][:])
+            bank = psum.tile([P, width(cols)], F32, name=f"back{c}", tag=back_tags[c])
+            for block in spans(0, (P,) * (width(cols) // P)):
+                nc.tensor.transpose(bank[:, block], staged[:, block], identity[:])
+            back.append(bank)
+
+        partial = []
+        for c in range(len(PLAIN_CHUNKS) + 1):
+            if c < len(PLAIN_CHUNKS):
+                cols = PLAIN_CHUNKS[c]
+                part = sb.tile([P, width(cols)], F32, name=f"partial{c}")
+                nc.vector.scalar_tensor_tensor(
+                    part[:], old_plain[:, cols], fade_sb[:], vector_window[:, cols], ALU.mult, ALU.add
+                )
+                partial.append(part)
+            if c > 0:
+                cols = PLAIN_CHUNKS[c - 1]
+                result = sb.tile([P, width(cols)], F32, name=f"plain_result{c - 1}")
+                nc.vector.tensor_tensor(result[:], partial[c - 1][:], scalar_window[:, cols], ALU.add)
+                nc.sync.dma_start(out[:, cols], result[:])
+
+        for c, cols in enumerate(TURNED_CHUNKS):
+            result = sb.tile([P, width(cols)], F32, name=f"turned_result{c}")
+            nc.vector.tensor_tensor(result[:], back[c][:], vector_window[:, cols], ALU.add)
             nc.sync.dma_start(out[:, cols], result[:])

from contextlib import ExitStack

import concourse.mybir as mybir
from concourse.masks import make_identity

F32 = mybir.dt.float32
BF16 = mybir.dt.bfloat16
I32 = mybir.dt.int32
U32 = mybir.dt.uint32
U16 = mybir.dt.uint16
U8 = mybir.dt.uint8
FP8X4 = mybir.dt.float8_e4m3fn_x4
ALU = mybir.AluOpType
ACT = mybir.ActivationFunctionType
AXIS = mybir.AxisListType

P = 128
PACK = 4
ENTRIES = 16
QUADRANT = 32
D, T, I, Q, J, G, M = 512, 2048, 512, 128, 512, 64, 2048
RUN = I // G
WEIGHT_SCALE = 512.0
FLOPS = 2 * D * J * Q + 2 * J * Q * I + 2 * D * Q * I


def spans(first, widths):
    return [slice(first + sum(widths[:c]), first + sum(widths[: c + 1])) for c in range(len(widths))]


SLOT_HALVES = spans(0, (I // 2, I // 2))
RUN_HALVES = spans(0, (G // 2, G // 2))
MIXER_CHUNKS = spans(0, (256, 128, 128))
PLAIN_CHUNKS = spans(0, (128, 384, 512))
PLAIN_COLS = PLAIN_CHUNKS[-1].stop
TURNED_CHUNKS = spans(PLAIN_COLS, (256, 256, 256, 256))
FADED_PIECES = spans(PLAIN_COLS, (512, 512))


def width(cols):
    return cols.stop - cols.start


def interleave(engine_copy, dst, src):
    engine_copy(
        out=dst.rearrange("p (c i) t -> p c t i", i=4),
        in_=src.rearrange("p t (c i) -> p c t i", i=4),
    )


def tile_attend_mixedslots_runcap_counts_kernel(
    tc, query, keys_words, keys_scales, hf, mixer, cap, old, fade, offs, offs2, offs3, out
):
    nc = tc.nc
    with ExitStack() as ctx:
        lists = ctx.enter_context(tc.tile_pool(name="lists", bufs=1))
        sb = ctx.enter_context(tc.tile_pool(name="sb", bufs=1))
        reused = ctx.enter_context(tc.tile_pool(name="reused", bufs=1))
        psum = ctx.enter_context(tc.psum_pool(name="psum", bufs=1))

        def quantise(words, scales, interleaved):
            nc.vector.quantize_mx(
                out=words.bitcast(FP8X4), scales=scales, in_=interleaved.rearrange("p c t -> p (c t)")
            )

        def multiply(bank, lhs_words, lhs_scales, rhs_words, rhs_scales, start, stop):
            nc.tensor.matmul_mx(
                out=bank,
                lhsT=lhs_words.bitcast(FP8X4),
                lhsT_scale=lhs_scales,
                rhs=rhs_words.bitcast(FP8X4),
                rhs_scale=rhs_scales,
                start=start,
                stop=stop,
            )

        slot_list = lists.tile([P, I // ENTRIES], U16, name="slot_list")
        mixed_list = lists.tile([P, J // ENTRIES], U16, name="mixed_list")
        place_list = lists.tile([P, I // ENTRIES], U16, name="place_list")

        pool_scales = sb.tile([P, T], U8, name="pool_scales", align_bytes=64)
        pool_words = sb.tile([P, T], U32, name="pool_words", align_bytes=64)
        vector_window = sb.tile([P, M], F32, name="vector_window")
        identity = sb.tile([P, P], F32, name="identity")
        nc.vector.memset(pool_scales[:].bitcast(I32), 0)
        nc.vector.memset(identity[:], 0.0)
        make_identity(nc, identity[:], nomemset=True)
        nc.vector.memset(vector_window[:], 0.0)

        query_raw = sb.tile([P, PACK, Q], F32, name="query_raw")
        nc.sync.dma_start(query_raw[:], query.rearrange("(p t) q -> p t q", t=PACK))
        nc.sync.dma_start(mixed_list[:], offs2)
        nc.sync.dma_start(slot_list[:], offs)
        for r in range(4):
            nc.sync.dma_start(pool_scales[r:P:QUADRANT, :].bitcast(I32), keys_scales[0, r:16:4, :].bitcast(I32))
        nc.sync.dma_start(
            pool_words[:].bitcast(I32), keys_words[0].rearrange("p n t -> p (n t)").bitcast(I32)
        )
        hf_sb = sb.tile([P, PACK], F32, name="hf_sb")
        nc.sync.dma_start(hf_sb[:], hf.rearrange("(p t) o -> p (t o)", t=PACK))
        mixer_rows = mixer.rearrange("(p t) i -> p t i", t=PACK)
        mixer_raw = []
        for c, cols in enumerate(MIXER_CHUNKS):
            chunk = sb.tile([P, PACK, width(cols)], F32, name=f"mixer_raw{c}")
            nc.sync.dma_start(chunk[:], mixer_rows[:, :, cols])
            mixer_raw.append(chunk)
        cap_sb = sb.tile([P, 1], F32, name="cap_sb")
        fade_sb = sb.tile([P, 1], F32, name="fade_sb")
        old_plain = sb.tile([P, PLAIN_COLS], F32, name="old_plain")
        old_turned = [sb.tile([P, width(cols)], F32, name=f"old_turned{h}") for h, cols in enumerate(FADED_PIECES)]
        nc.sync.dma_start(fade_sb[:], fade)
        nc.sync.dma_start(old_turned[0][:], old[:, FADED_PIECES[0]])
        nc.sync.dma_start(cap_sb[:], cap)
        nc.sync.dma_start(old_turned[1][:], old[:, FADED_PIECES[1]])
        nc.sync.dma_start(place_list[:], offs3)
        nc.sync.dma_start(old_plain[:], old[:, :PLAIN_COLS])

        query_bf = sb.tile([P, Q, PACK], BF16, name="query_bf", align_bytes=64)
        query_words = sb.tile([P, Q], U32, name="query_words", align_bytes=64)
        query_scales = sb.tile([P, Q], U8, name="query_scales", align_bytes=64)
        interleave(nc.vector.tensor_copy, query_bf[:], query_raw[:])
        quantise(query_words[:], query_scales[:], query_bf[:])

        mixed_words = sb.tile([P, J], U32, name="mixed_words", align_bytes=64)
        mixed_scales = sb.tile([P, J], U8, name="mixed_scales", align_bytes=64)
        slot_words = sb.tile([P, I], U32, name="slot_words", align_bytes=64)
        slot_scales = sb.tile([P, I], U8, name="slot_scales", align_bytes=64)
        nc.vector.tensor_copy(
            mixed_scales[:].rearrange("p (t m) -> p m t", t=PACK), pool_scales[:].indirect(mixed_list[:])
        )
        nc.vector.tensor_copy(slot_scales[:], pool_scales[:].indirect(slot_list[:]))
        nc.vector.tensor_copy(
            mixed_words[:].rearrange("p (t m) -> p m t", t=PACK), pool_words[:].indirect(mixed_list[:])
        )
        a0 = psum.tile([P, PACK, Q], F32, name="a0", tag="a0")
        for t, cols in enumerate(spans(0, (P,) * PACK)):
            multiply(
                a0[:, t, :], mixed_words[:, cols], mixed_scales[:, cols], query_words[:], query_scales[:], True, True
            )
        nc.vector.tensor_copy(slot_words[:], pool_words[:].indirect(slot_list[:]))

        scores = [psum.tile([P, I // 2], F32, name=f"scores{h}", tag=f"scores{h}") for h in range(2)]
        for h, cols in enumerate(SLOT_HALVES):
            multiply(
                scores[h][:], query_words[:], query_scales[:], slot_words[:, cols], slot_scales[:, cols], True, False
            )

        af_bf = sb.tile([P, Q, PACK], BF16, name="af_bf", align_bytes=64)
        af_scales = sb.tile([P, Q], U8, name="af_scales", align_bytes=64)
        nc.vector.tensor_tensor(
            af_bf[:],
            a0[:].rearrange("p t q -> p q t"),
            hf_sb[:].unsqueeze(1).to_broadcast([P, Q, PACK]),
            ALU.mult,
        )

        mixer_bf = [
            sb.tile([P, width(MIXER_CHUNKS[0]), PACK], BF16, name="mixer_bf0", tag="mixer_bf0", align_bytes=64),
            sb.tile([P, width(MIXER_CHUNKS[1]), PACK], BF16, name="mixer_bf1", align_bytes=64),
            reused.tile([P, width(MIXER_CHUNKS[2]), PACK], BF16, name="mixer_bf2", align_bytes=64, offset=0),
        ]
        mixer_words = sb.tile([P, I], U32, name="mixer_words", align_bytes=64)
        mixer_scales = sb.tile([P, I], U8, name="mixer_scales", align_bytes=64)
        for c in range(len(MIXER_CHUNKS)):
            interleave(nc.scalar.copy, mixer_bf[c][:], mixer_raw[c][:])

        quantise(mixer_words[:, MIXER_CHUNKS[0]], mixer_scales[:, MIXER_CHUNKS[0]], mixer_bf[0][:])
        af_words = sb.tile([P, Q], U32, name="af_words", tag="mixer_bf0", align_bytes=64)
        quantise(af_words[:], af_scales[:], af_bf[:])
        for c in range(1, len(MIXER_CHUNKS)):
            quantise(mixer_words[:, MIXER_CHUNKS[c]], mixer_scales[:, MIXER_CHUNKS[c]], mixer_bf[c][:])
        for cols in MIXER_CHUNKS:
            h, first = divmod(cols.start, I // 2)
            multiply(
                scores[h][:, first : first + width(cols)],
                af_words[:],
                af_scales[:],
                mixer_words[:, cols],
                mixer_scales[:, cols],
                False,
                cols.stop == SLOT_HALVES[h].stop,
            )

        scalar_window = reused.tile([P, M], F32, name="scalar_window", align_bytes=64, offset=64)
        nc.gpsimd.memset(scalar_window[:], 0.0)

        cap_scaled = sb.tile([P, 1], F32, name="cap_scaled")
        nc.scalar.activation(cap_scaled[:], cap_sb[:], ACT.Copy, scale=WEIGHT_SCALE)
        neg_first_max = reused.tile([P, 1], F32, name="neg_first_max", align_bytes=64, offset=0)
        neg_max = sb.tile([P, 1], F32, name="neg_max")
        neg_scores = sb.tile([P, I // 2], F32, name="neg_scores")
        nc.vector.tensor_reduce(neg_first_max[:], scores[0][:], AXIS.X, ALU.max, negate=True)
        nc.vector.tensor_scalar(
            neg_scores[:], scores[1][:], -1.0, neg_first_max[:], ALU.mult, ALU.min, accum_out=neg_max[:]
        )
        p = sb.tile([P, I], F32, name="p")
        run_sums = sb.tile([P, G], F32, name="run_sums")
        half_sums = [sb.tile([P, 1], F32, name=f"half_sum{h}") for h in range(2)]
        for h, (source, sign) in enumerate(((scores[0], 1.0), (neg_scores, -1.0))):
            nc.scalar.activation(
                p[:, SLOT_HALVES[h]], source[:], ACT.Exp, scale=sign, bias=neg_max[:], accum_out=half_sums[h][:]
            )
            nc.vector.tensor_reduce(
                run_sums[:, RUN_HALVES[h]],
                p[:, SLOT_HALVES[h]].rearrange("p (g r) -> p g r", r=RUN),
                AXIS.X,
                ALU.add,
            )
        first_share = sb.tile([P, 1], F32, name="first_share", tag="first_share")
        row_share = sb.tile([P, 1], F32, name="row_share")
        nc.scalar.activation(first_share[:], half_sums[0][:], ACT.Copy, scale=1.0 / WEIGHT_SCALE)
        nc.scalar.activation(
            row_share[:], half_sums[1][:], ACT.Identity, scale=1.0 / WEIGHT_SCALE, bias=first_share[:]
        )

        faded = [
            sb.tile([P, width(FADED_PIECES[0])], F32, name="faded0"),
            sb.tile([P, width(FADED_PIECES[1])], F32, name="faded1", tag="first_share"),
        ]
        for h in range(2):
            nc.scalar.activation(faded[h][:], old_turned[h][:], ACT.Copy, scale=fade_sb[:])

        turned_tags = ("turned0", "turned1", "a0", "scores1")
        back_tags = ("back0", "back1", "back2", "scores0")
        turned = [
            psum.tile([P, width(cols)], F32, name=f"turned{c}", tag=turned_tags[c])
            for c, cols in enumerate(TURNED_CHUNKS)
        ]

        def add_turned(c, source, first_col, opens):
            blocks = width(TURNED_CHUNKS[c]) // P
            for b in range(blocks):
                col = first_col + b * P
                nc.tensor.matmul(
                    turned[c][:, b * P : (b + 1) * P],
                    source[:, col : col + P],
                    identity[:],
                    start=opens and b == 0,
                    stop=not opens and b == blocks - 1,
                    is_transpose=True,
                )

        for c, cols in enumerate(TURNED_CHUNKS):
            h, first_col = divmod(cols.start - PLAIN_COLS, width(FADED_PIECES[0]))
            add_turned(c, faded[h], first_col, True)

        inverse_run = sb.tile([P, G], F32, name="inverse_run")
        inverse_row = sb.tile([P, 1], F32, name="inverse_row")
        nc.vector.reciprocal(inverse_run[:, RUN_HALVES[0]], run_sums[:, RUN_HALVES[0]])
        nc.vector.reciprocal(inverse_row[:], row_share[:])
        nc.vector.reciprocal(inverse_run[:, RUN_HALVES[1]], run_sums[:, RUN_HALVES[1]])
        first_factor = sb.tile([P, G // 2], F32, name="first_factor")
        first_ws = sb.tile([P, I // 2], F32, name="first_ws")
        second_factor = sb.tile([P, I // 2], F32, name="second_factor")
        nc.vector.tensor_scalar(
            first_factor[:], inverse_run[:, RUN_HALVES[0]], cap_scaled[:], inverse_row[:], ALU.mult, ALU.min
        )
        nc.vector.tensor_scalar(
            second_factor[:].rearrange("p (g r) -> p g r", r=RUN),
            inverse_run[:, RUN_HALVES[1]].unsqueeze(2).to_broadcast([P, G // 2, RUN]),
            cap_scaled[:],
            inverse_row[:],
            ALU.mult,
            ALU.min,
        )
        nc.vector.tensor_tensor(
            first_ws[:].rearrange("p (g r) -> p g r", r=RUN),
            p[:, SLOT_HALVES[0]].rearrange("p (g r) -> p g r", r=RUN),
            first_factor[:].unsqueeze(2).to_broadcast([P, G // 2, RUN]),
            ALU.mult,
        )
        half_list = I // 2 // ENTRIES
        nc.scalar.activation(scalar_window[:].indirect(place_list[:, :half_list]), first_ws[:], ACT.Copy)
        nc.vector.tensor_tensor(
            vector_window[:].indirect(place_list[:, half_list:]), p[:, SLOT_HALVES[1]], second_factor[:], ALU.mult
        )

        for c, cols in enumerate(TURNED_CHUNKS):
            add_turned(c, scalar_window, cols.start, False)
        back = []
        for c, cols in enumerate(TURNED_CHUNKS):
            staged = sb.tile([P, width(cols)], F32, name=f"staged{c}")
            nc.scalar.copy(staged[:], turned[c][:])
            bank = psum.tile([P, width(cols)], F32, name=f"back{c}", tag=back_tags[c])
            for block in spans(0, (P,) * (width(cols) // P)):
                nc.tensor.transpose(bank[:, block], staged[:, block], identity[:])
            back.append(bank)

        partial = []
        for c in range(len(PLAIN_CHUNKS) + 1):
            if c < len(PLAIN_CHUNKS):
                cols = PLAIN_CHUNKS[c]
                part = sb.tile([P, width(cols)], F32, name=f"partial{c}")
                nc.vector.scalar_tensor_tensor(
                    part[:], old_plain[:, cols], fade_sb[:], vector_window[:, cols], ALU.mult, ALU.add
                )
                partial.append(part)
            if c > 0:
                cols = PLAIN_CHUNKS[c - 1]
                result = sb.tile([P, width(cols)], F32, name=f"plain_result{c - 1}")
                nc.vector.tensor_tensor(result[:], partial[c - 1][:], scalar_window[:, cols], ALU.add)
                nc.sync.dma_start(out[:, cols], result[:])

        for c, cols in enumerate(TURNED_CHUNKS):
            result = sb.tile([P, width(cols)], F32, name=f"turned_result{c}")
            nc.vector.tensor_tensor(result[:], back[c][:], vector_window[:, cols], ALU.add)
            nc.sync.dma_start(out[:, cols], result[:])
